import numpy as np
import ml_dtypes


def mxq(x, axis, fmt="e4m3"):
    dtype, down = {"e4m3": (ml_dtypes.float8_e4m3fn, 7), "e5m2": (ml_dtypes.float8_e5m2, 14)}[fmt]
    v = np.moveaxis(np.asarray(x, np.float32).astype(ml_dtypes.bfloat16).astype(np.float64), axis, -1)
    blocks = v.reshape(v.shape[:-1] + (-1, 32))
    amax = np.abs(blocks).max(-1, keepdims=True)
    byte = np.maximum(np.where(amax > 0, np.frexp(amax)[1] - 1 + 127, 0) - down, 1)
    scale = np.exp2(byte - 127.0)
    codes = (blocks / scale).astype(np.float32).astype(dtype).astype(np.float64)
    return np.moveaxis((codes * scale).reshape(v.shape), -1, axis)


WIDE = False


def mx_kscale(k):
    if not WIDE:
        return np.ones(k)
    levels = np.array([10, -10, 5, -5, 0])
    if k % 512:
        return np.exp2(np.random.permutation(np.resize(levels, k // 32))).repeat(32)
    a = np.empty((k // 512, 16))
    for p in range(k // 512):
        a[p, :8] = np.random.permutation(np.resize(levels, 8))
        for g in range(8):
            far = levels[np.abs(levels - a[p, g]) >= 10]
            a[p, g + 8] = far[np.random.randint(len(far))]
    return np.exp2(a.ravel()).repeat(32)


def f64(x):
    return np.asarray(x).astype(np.float64)


def striped(idx):
    return np.tile(idx.reshape(-1, 16).T, (8, 1)).astype(np.uint16)


def unstriped(offs):
    return offs[:16].T.reshape(-1).astype(np.int64)


E2M1 = np.array([0.0, 0.5, 1.0, 1.5, 2.0, 3.0, 4.0, 6.0, -0.0, -0.5, -1.0, -1.5, -2.0, -3.0, -4.0, -6.0])


def pack_weight(w, fmt):
    k, n = w.shape
    w = f64(np.asarray(w, np.float32).astype(ml_dtypes.bfloat16)).reshape(k // 32, 32, n)
    amax = np.abs(w).max(1)
    if fmt == "e4m3":
        byte = np.frexp(amax)[1] - 1 + 127 - 7
    else:
        mant, ex = np.frexp(amax / 6.0)
        byte = np.where(mant > 0.5, ex, ex - 1) + 127
    byte = np.clip(np.where(amax > 0, byte, 1), 1, 254)
    scaled = (w * np.exp2(127.0 - byte)[:, None, :]).reshape(k, n).astype(np.float32)
    by_word = np.ascontiguousarray(scaled.reshape(k // 512, 128, 4, n).transpose(0, 1, 3, 2))
    if fmt == "e4m3":
        words = by_word.astype(ml_dtypes.float8_e4m3fn).view(np.uint8)
    else:
        c = by_word.astype(ml_dtypes.float4_e2m1fn).view(np.uint8) & 0xF
        words = (c[..., 0::2] | (c[..., 1::2] << 4)).reshape(k // 512, 128, 2 * n)
    return np.ascontiguousarray(words), np.ascontiguousarray(byte.astype(np.uint8).reshape(k // 512, 16, n))


def unpack_weight(words, scales, fmt):
    g, _, n = scales.shape
    words = np.ascontiguousarray(words).reshape(g, 128, n, -1)
    if fmt == "e4m3":
        vals = words.view(ml_dtypes.float8_e4m3fn).astype(np.float64)
    else:
        nib = np.empty((g, 128, n, 4), np.uint8)
        nib[..., 0::2] = words & 0xF
        nib[..., 1::2] = words >> 4
        vals = E2M1[nib]
    vals = vals * np.repeat(np.exp2(scales.astype(np.float64) - 127.0), 8, axis=1)[..., None]
    return vals.transpose(0, 1, 3, 2).reshape(g * 512, n)


def relu(v):
    return np.maximum(v, 0.0)


K, T, E, H, N = 512, 768, 8, 512, 256
COUNTS = (128, 128, 128, 128, 128, 256, 512, 128)
STARTS = np.cumsum((0,) + COUNTS)


def by_expert(wq, xq):
    return np.concatenate([wq[e].T @ xq[:, STARTS[e]:STARTS[e + 1]] for e in range(E)], axis=1)


def setup_inputs():
    n = np.random.standard_normal
    s = mx_kscale(K)[:, None]
    u = mx_kscale(H)
    both = np.repeat(np.arange(E), COUNTS)
    pair = np.stack([both[:T], both[T:]])[:, np.random.permutation(T)]
    pair = np.where(np.random.rand(T) < 0.5, pair, pair[::-1])
    for _ in range(8):
        s_, t_ = np.random.permutation(T).reshape(2, -1); r = np.random.randint(2, size=T // 2); q = np.random.randint(2, size=T // 2); x, y = pair[r, s_].copy(), pair[q, t_].copy()
        ok = (pair[1 - r, s_] != y) & (pair[1 - q, t_] != x); pair[r[ok], s_[ok]] = y[ok]; pair[q[ok], t_[ok]] = x[ok]
    order = np.argsort(pair.reshape(-1), kind="stable")
    slot_token = order % T; pos = np.empty(2 * T, np.int64); pos[order] = np.arange(2 * T); pos = pos.reshape(2, T)
    g = np.random.uniform(0.2, 0.8, T)
    w1 = [pack_weight(m, "e2m1") for m in n((E, K, H)) / np.sqrt(K) / s[None]]
    w3 = [pack_weight(m, "e2m1") for m in n((E, K, H)) / np.sqrt(K) / s[None] * u[None, None, :]]
    w2 = [pack_weight(m, "e2m1") for m in n((E, H, N)) / np.sqrt(H) / u[None, :, None]]
    x = pack_weight(n((K, T)) * s, "e4m3")
    return {
        "x_words": x[0],
        "x_scales": x[1],
        "w1_words": np.stack([m[0] for m in w1]),
        "w1_scales": np.stack([m[1] for m in w1]),
        "w3_words": np.stack([m[0] for m in w3]),
        "w3_scales": np.stack([m[1] for m in w3]),
        "w2_words": np.stack([m[0] for m in w2]),
        "w2_scales": np.stack([m[1] for m in w2]),
        "gate": np.stack([np.tile(g, (N, 1)), np.tile(1.0 - g, (N, 1))]).astype(np.float32),
        "offs": striped(slot_token),
        "pos1": striped(pos[0]),
        "pos2": striped(pos[1]),
    }


def reference(x_words, x_scales, w1_words, w1_scales, w3_words, w3_scales, w2_words, w2_scales, gate, offs, pos1, pos2):
    idx = unstriped(offs)
    w1 = np.stack([unpack_weight(w1_words[e], w1_scales[e], "e2m1") for e in range(E)])
    w3 = np.stack([unpack_weight(w3_words[e], w3_scales[e], "e2m1") for e in range(E)])
    w2 = np.stack([unpack_weight(w2_words[e], w2_scales[e], "e2m1") for e in range(E)])
    xq = unpack_weight(x_words, x_scales, "e4m3")[:, idx]
    h = relu(by_expert(w1, xq))
    h = h * by_expert(w3, xq)
    y = by_expert(w2, mxq(h, 0, "e4m3"))
    return f64(gate[0]) * y[:, unstriped(pos1)] + f64(gate[1]) * y[:, unstriped(pos2)]

@@ -1,0 +1,229 @@
+from contextlib import ExitStack
+
+import concourse.mybir as mybir
+from concourse.masks import make_identity
+
+K, T, E, H, N = 512, 768, 8, 512, 256
+COUNTS = (128, 128, 128, 128, 128, 256, 512, 128)
+S = sum(COUNTS)
+FLOPS = 2 * S * (2 * K * H + H * N)
+
+F32 = mybir.dt.float32
+BF16 = mybir.dt.bfloat16
+I32 = mybir.dt.int32
+U32 = mybir.dt.uint32
+U16 = mybir.dt.uint16
+U8 = mybir.dt.uint8
+FP8X4 = mybir.dt.float8_e4m3fn_x4
+FP4X4 = mybir.dt.float4_e2m1fn_x4
+MULT = mybir.AluOpType.mult
+ADD = mybir.AluOpType.add
+RELU = mybir.ActivationFunctionType.Relu
+
+P = 128
+EXPERT_OF_TILE = [e for e in range(E) for c in range(COUNTS[e] // P)]
+CFG = {"groups":[[7,8],[9,10],[5,6],[11],[0,1],[2,3],[4]],"pieces":[[[7],[8]],[[9,10]],[[5,6]],[[11]],[[0,1]],[[2,3]],[[4]]],"combine":[[0,0,768],[1,0,384],[1,384,768]],"zero":[["s1a","v"],["xs","v"],["s3a","v"],["s2","g"],["s1b","v"],["s3b","g"]],"early":[["xs","s"],["w1a","s"],["w3a","s"],["s1a","a"],["s3a","a"],["w2a","s"],["s2","s"],["w1b","s"],["w3b","s"],["s1b","s"],["s3b","a"]],"late":[["w1c","a"],["w3c","s"],["w2c","s"],["gates","s"]],"xg":3,"sg":8,"a":2,"b":3,"t":1,"y":2,"tv":[0,0,0,1,0,0,0],"yv":[0,0,0,0,0,0,0],"ytag":["y","y"],"ga":2,"pl":1,"order":["l","t","p","g"],"tail":[[0,0],[1,0],[0,1],[2,0],[1,1],[0,2],[1,2],[2,1],[2,2]]}
+GROUPS = CFG["groups"]
+PIECES = CFG["pieces"]
+COMBINE = CFG["combine"]
+
+
+def tile_moe_rag_glu_relu_kernel(
+    tc, x_words, x_scales, w1_words, w1_scales, w3_words, w3_scales, w2_words, w2_scales, gate, offs, pos1, pos2, out
+):
+    nc = tc.nc
+    with ExitStack() as ctx:
+        keep = ctx.enter_context(tc.tile_pool(name="keep", bufs=1))
+        ring = ctx.enter_context(tc.tile_pool(name="ring", bufs=3))
+        psum = ctx.enter_context(tc.psum_pool(name="psum", bufs=1))
+
+        def zeroed_plane(engine, name, experts, width):
+            plane = keep.tile([P, experts, width], U8, name=name, align_bytes=64)
+            engine.memset(plane[:].bitcast(I32), 0)
+            return plane
+
+        def load_plane(queue, plane, scales):
+            for r in range(4):
+                queue.dma_start(
+                    plane[:].bitcast(I32)[r:P:32, :, :],
+                    scales[:, r:16:4, :].rearrange("e q c -> q e c").bitcast(I32),
+                )
+
+        def load_words(queue, name, words, tag=""):
+            tile = keep.tile([P, words.shape[0], words.shape[2]], U8, name=name, tag=tag, align_bytes=64)
+            queue.dma_start(tile[:].bitcast(I32), words.rearrange("e p c -> p e c").bitcast(I32))
+            return tile
+
+        warm = keep.tile([P, 2], F32, name="warm")
+        nc.vector.memset(warm[:, 0:1], 0.0)
+        nc.scalar.activation(warm[:, 1:2], warm[:, 0:1], RELU)
+        eng = {"v": nc.vector, "g": nc.gpsimd, "s": nc.sync, "a": nc.scalar}
+        planes = {}
+        for name, e in CFG["zero"]:
+            if name == "xs":
+                xs = keep.tile([P, T], U8, name="xs", align_bytes=64)
+                eng[e].memset(xs[:].bitcast(I32), 0)
+            else:
+                planes[name] = zeroed_plane(eng[e], name, {"s1a": 3, "s3a": 3, "s2": E, "s1b": 5, "s3b": 5}[name], N if name == "s2" else H)
+        s1a, s3a, s2, s1b, s3b = [planes[k] for k in ("s1a", "s3a", "s2", "s1b", "s3b")]
+        ident = keep.tile([P, P], F32, name="ident")
+        make_identity(nc, ident[:])
+
+        offs_t = keep.tile([P, S // 16], U16, name="offs_t")
+        nc.sync.dma_start(offs_t[:], offs)
+        xw = keep.tile([P, T], I32, name="xw", align_bytes=64)
+        nc.sync.dma_start(xw[:], x_words[0].rearrange("p t r -> p (t r)").bitcast(I32))
+        plane_src = {"s1a": w1_scales[5:8, 0], "s3a": w3_scales[5:8, 0], "s2": w2_scales[:, 0], "s1b": w1_scales[0:5, 0], "s3b": w3_scales[0:5, 0]}
+        word_src = {"w1a": w1_words[6:7, 0], "w3a": w3_words[6:7, 0], "w2a": w2_words[5:8, 0], "w1b": w1_words[5:8:2, 0], "w3b": w3_words[5:8:2, 0],
+                    "w1c": w1_words[0:5, 0], "w3c": w3_words[0:5, 0], "w2c": w2_words[0:5, 0]}
+        W = {}
+        def load(name, e, tag=""):
+            if name == "xs":
+                for r in range(4):
+                    eng[e].dma_start(xs[:].bitcast(I32)[r:P:32, :], x_scales[0, r:16:4, :].bitcast(I32))
+            elif name in plane_src:
+                load_plane(eng[e], planes[name], plane_src[name])
+            elif name == "gates":
+                W[name] = keep.tile([P, 2, 2, T], F32, name="gates", tag=tag, align_bytes=64)
+                eng[e].dma_start(W[name][:].rearrange("p c h t -> p (c h) t"), gate.rearrange("c (h p) t -> p (c h) t", p=P))
+            else:
+                W[name] = load_words(eng[e], name, word_src[name], tag)
+        for name, e in CFG["early"]:
+            load(name, e)
+
+        def first_layer(e):
+            if e == 6:
+                return (W["w1a"][:, 0, :], s1a[:, 1, :]), (W["w3a"][:, 0, :], s3a[:, 1, :])
+            if e >= 5:
+                return (W["w1b"][:, (e - 5) // 2, :], s1a[:, e - 5, :]), (W["w3b"][:, (e - 5) // 2, :], s3a[:, e - 5, :])
+            return (W["w1c"][:, e, :], s1b[:, e, :]), (W["w3c"][:, e, :], s3b[:, e, :])
+
+        def second_layer(e, half):
+            words = W["w2a"][:, e - 5, :] if e >= 5 else W["w2c"][:, e, :]
+            return words[:, 2 * P * half : 2 * P * (half + 1)], s2[:, e, P * half : P * (half + 1)]
+
+        y = [keep.tile([P, S], F32, name="y%d" % half) for half in range(2)]
+        tokens = {}
+        hidden = {}
+        order = [s for group in GROUPS for s in group]
+
+        def gather(g):
+            for piece in PIECES[g]:
+                n = P * len(piece)
+                cut = offs_t[:, 8 * piece[0] : 8 * piece[0] + n // 16]
+                words = ring.tile([P, n], U32, name="xg", bufs=CFG["xg"], align_bytes=64)
+                scales = ring.tile([P, n], U8, name="sg", bufs=CFG["sg"], align_bytes=64)
+                nc.vector.tensor_copy(words[:], xw[:].bitcast(U32).indirect(cut))
+                nc.vector.tensor_copy(scales[:], xs[:].indirect(cut))
+                for c, s in enumerate(piece):
+                    tokens[s] = (words[:, P * c : P * (c + 1)], scales[:, P * c : P * (c + 1)])
+
+        def gated(g):
+            for s in GROUPS[g]:
+                words, scales = tokens[s]
+                a = psum.tile([P, H], F32, name="a", bufs=CFG["a"])
+                b = psum.tile([P, H], F32, name="b", bufs=CFG["b"])
+                for acc, (w, ws) in zip((a, b), first_layer(EXPERT_OF_TILE[s])):
+                    nc.tensor.matmul_mx(
+                        out=acc[:], lhsT=words.bitcast(FP8X4), lhsT_scale=scales,
+                        rhs=w.bitcast(FP4X4), rhs_scale=ws, start=True, stop=True,
+                    )
+                place = order.index(s)
+                if place < len(CFG["late"]):
+                    ra = keep.tile([P, H], F32, name="ra", tag="late%d" % place, align_bytes=64)
+                else:
+                    ra = ring.tile([P, H], F32, name="ra")
+                nc.scalar.activation(
+                    ra[:].rearrange("r (u p e) -> r u p e", u=2, e=2),
+                    a[:].rearrange("r (p u e) -> r u p e", u=2, e=2),
+                    RELU,
+                )
+                h = ring.tile([P, H], BF16, name="h", bufs=4)
+                nc.vector.tensor_tensor(
+                    h[:].rearrange("r (u p e) -> r u p e", u=2, e=2),
+                    b[:].rearrange("r (p u e) -> r u p e", u=2, e=2),
+                    ra[:].rearrange("r (u p e) -> r u p e", u=2, e=2),
+                    MULT,
+                )
+                hidden[s] = h
+
+        def turn(g):
+            m = len(GROUPS[g])
+            turned = psum.tile([P, m, 2, P], F32, name="turned", bufs=CFG["t"])
+            for c, s in enumerate(GROUPS[g]):
+                pairs = hidden[s][:].bitcast(F32)
+                for u in range(2):
+                    nc.tensor.transpose(turned[:, c, u, :], pairs[:, P * u : P * (u + 1)], ident[:])
+            grouped = ring.tile([P, m * P * 4], BF16, name="grouped", align_bytes=64)
+            (nc.vector.tensor_copy if CFG["tv"][g] else nc.scalar.copy)(
+                grouped[:].bitcast(F32).rearrange("p (c r u) -> p c r u", c=m, u=2),
+                turned[:].rearrange("p c u r -> p c r u"),
+            )
+            codes = ring.tile([P, m * P], U32, name="codes", align_bytes=64)
+            scales = ring.tile([P, m * P], U8, name="scales", align_bytes=64)
+            nc.vector.quantize_mx(out=codes[:].bitcast(FP8X4), scales=scales[:], in_=grouped[:])
+            return codes, scales
+
+        def project(g, codes, scales):
+            group = GROUPS[g]
+            m = len(group)
+            if CFG["yv"][g]:
+                acc = [psum.tile([P, m * P], F32, name="acc", tag=CFG["ytag"][half], bufs=CFG[CFG["ytag"][half]])[:] for half in range(2)]
+            else:
+                both = psum.tile([P, 2, m * P], F32, name="acc", tag="y", bufs=CFG["y"])
+                acc = [both[:, half, :] for half in range(2)]
+            same = len(set(EXPERT_OF_TILE[s] for s in group)) == 1
+            runs = [(group[0], 0, m * P)] if same else [(s, c * P, (c + 1) * P) for c, s in enumerate(group)]
+            for half in range(2):
+                for s, lo, hi in runs:
+                    w, ws = second_layer(EXPERT_OF_TILE[s], half)
+                    nc.tensor.matmul_mx(
+                        out=acc[half][:, lo:hi], lhsT=w.bitcast(FP4X4), lhsT_scale=ws,
+                        rhs=codes[:, lo:hi].bitcast(FP8X4), rhs_scale=scales[:, lo:hi], start=True, stop=True,
+                    )
+            for half in range(2):
+                (nc.vector.tensor_copy if CFG["yv"][g] in (half + 1, 3) else nc.scalar.copy)(y[half][:, P * group[0] : P * (group[0] + m)], acc[half])
+
+        G = len(GROUPS)
+        made = {}
+        done_late = 0
+        for step in range(-CFG["ga"], G + 2):
+            for what in CFG["order"]:
+                if what == "g" and 0 <= step + CFG["ga"] < G:
+                    gather(step + CFG["ga"])
+                if what == "l" and 0 <= step + 1 < G:
+                    gated(step + 1)
+                    while done_late < len(CFG["late"]) and order[done_late] in hidden:
+                        load(CFG["late"][done_late][0], CFG["late"][done_late][1], "late%d" % done_late)
+                        done_late += 1
+                if what == "t" and 0 <= step < G:
+                    made[step] = turn(step)
+                if what == "p" and 0 <= step - CFG["pl"] < G:
+                    project(step - CFG["pl"], *made[step - CFG["pl"]])
+
+        pos_t = []
+        for name, pos in (("pos1_t", pos1), ("pos2_t", pos2)):
+            t = keep.tile([P, T // 16], U16, name=name)
+            nc.sync.dma_start(t[:], pos)
+            pos_t.append(t)
+
+        def weighted(i, choice):
+            half, lo, hi = COMBINE[i]
+            t = keep.tile([P, hi - lo], F32, name="term%d_%d" % (i, choice))
+            nc.vector.tensor_tensor(
+                t[:], y[half][:].indirect(pos_t[choice][:, lo // 16 : hi // 16]), W["gates"][:, choice, half, lo:hi], MULT
+            )
+            return t
+
+        def finish(i, terms):
+            half, lo, hi = COMBINE[i]
+            total = keep.tile([P, hi - lo], F32, name="total%d" % i)
+            nc.vector.tensor_tensor(total[:], terms[0][:], terms[1][:], ADD)
+            nc.sync.dma_start(out[P * half : P * (half + 1), lo:hi], total[:])
+
+        terms = {}
+        for kind, i in CFG["tail"]:
+            if kind == 2:
+                finish(i, (terms[i, 0], terms[i, 1]))
+            else:
+                terms[i, kind] = weighted(i, kind)

@@ -22,7 +22,7 @@ RELU = mybir.ActivationFunctionType.Relu
 
 P = 128
 EXPERT_OF_TILE = [e for e in range(E) for c in range(COUNTS[e] // P)]
-CFG = {"groups":[[7,8],[9,10],[5,6],[11],[0,1],[2,3],[4]],"pieces":[[[7],[8]],[[9,10]],[[5,6]],[[11]],[[0,1]],[[2,3]],[[4]]],"combine":[[0,0,768],[1,0,384],[1,384,768]],"zero":[["s1a","v"],["xs","v"],["s3a","v"],["s2","g"],["s1b","v"],["s3b","g"]],"early":[["xs","s"],["w1a","s"],["w3a","s"],["s1a","a"],["s3a","a"],["w2a","s"],["s2","s"],["w1b","s"],["w3b","s"],["s1b","s"],["s3b","a"]],"late":[["w1c","a"],["w3c","s"],["w2c","s"],["gates","s"]],"xg":3,"sg":8,"a":2,"b":3,"t":1,"y":2,"tv":[0,0,0,1,0,0,0],"yv":[0,0,0,0,0,0,0],"ytag":["y","y"],"ga":2,"pl":1,"order":["l","t","p","g"],"tail":[[0,0],[1,0],[0,1],[2,0],[1,1],[0,2],[1,2],[2,1],[2,2]]}
+CFG = {"combine":[[0,0,768],[1,0,384],[1,384,768]],"tail":[[0,0],[1,0],[0,1],[2,0],[1,1],[0,2],[1,2],[2,1],[2,2]],"xg":4,"sg":5,"a":2,"b":3,"t":1,"y":2,"ytag":["a","b"],"ga":4,"pl":6,"ll":2,"order":["t","g","l","p"],"pe_add":0,"groups":[[9,10],[7,8],[5,6],[11],[3,4],[1,2],[0]],"pieces":[[9],[10,11],[7,8],[5,6],[3,4],[1,2],[0]],"tv":[0,0,0,0,0,0,0],"yv":[0,3,0,0,3,3,0],"zero":[["s1",5,8,"v"],["xs",0,1,"v"],["s3",5,8,"v"],["s2",0,8,"v"],["s1",0,5,"g"],["s3",0,5,"v"]],"early":[["xw",0,0,1,"s"],["xs",0,1,1,"ssss"],["w1",6,7,1,"s"],["s3",5,8,1,"aaaa"],["w3",6,7,1,"s"],["s1",5,8,1,"aaaa"],["w2",5,8,1,"s"],["s2",0,8,1,"ssss"],["w3",5,8,2,"s"],["w1",5,8,2,"s"],["s1",0,5,1,"aaaa"],["s3",0,5,1,"aaaa"],["w1",0,5,1,"s"]],"late":[["w3",0,5,1,"s"],["w2",0,5,1,"s"],["gates",0,0,1,"s"]],"kind":"K","ra":6,"yb":["y","y","y","t","b","a","y"],"tb":["t","t","t","t","t","a","a"]}
 GROUPS = CFG["groups"]
 PIECES = CFG["pieces"]
 COMBINE = CFG["combine"]
@@ -37,14 +37,9 @@ def tile_moe_rag_glu_relu_kernel(
         ring = ctx.enter_context(tc.tile_pool(name="ring", bufs=3))
         psum = ctx.enter_context(tc.psum_pool(name="psum", bufs=1))
 
-        def zeroed_plane(engine, name, experts, width):
-            plane = keep.tile([P, experts, width], U8, name=name, align_bytes=64)
-            engine.memset(plane[:].bitcast(I32), 0)
-            return plane
-
         def load_plane(queue, plane, scales):
             for r in range(4):
-                queue.dma_start(
+                queue[r].dma_start(
                     plane[:].bitcast(I32)[r:P:32, :, :],
                     scales[:, r:16:4, :].rearrange("e q c -> q e c").bitcast(I32),
                 )
@@ -59,48 +54,46 @@ def tile_moe_rag_glu_relu_kernel(
         nc.scalar.activation(warm[:, 1:2], warm[:, 0:1], RELU)
         eng = {"v": nc.vector, "g": nc.gpsimd, "s": nc.sync, "a": nc.scalar}
         planes = {}
-        for name, e in CFG["zero"]:
-            if name == "xs":
-                xs = keep.tile([P, T], U8, name="xs", align_bytes=64)
-                eng[e].memset(xs[:].bitcast(I32), 0)
-            else:
-                planes[name] = zeroed_plane(eng[e], name, {"s1a": 3, "s3a": 3, "s2": E, "s1b": 5, "s3b": 5}[name], N if name == "s2" else H)
-        s1a, s3a, s2, s1b, s3b = [planes[k] for k in ("s1a", "s3a", "s2", "s1b", "s3b")]
+        plane_of = {}
+        for name, lo, hi, e in CFG["zero"]:
+            t = keep.tile([P, hi - lo, {"xs": T, "s1": H, "s3": H, "s2": N}[name]], U8, name="%s_%d" % (name, lo), align_bytes=64)
+            eng[e].memset(t[:].bitcast(I32), 0)
+            planes[name, lo] = t
+            for x in range(lo, hi):
+                plane_of[name, x] = t[:, x - lo, :]
+        xs = planes["xs", 0]
         ident = keep.tile([P, P], F32, name="ident")
         make_identity(nc, ident[:])
 
         offs_t = keep.tile([P, S // 16], U16, name="offs_t")
         nc.sync.dma_start(offs_t[:], offs)
         xw = keep.tile([P, T], I32, name="xw", align_bytes=64)
-        nc.sync.dma_start(xw[:], x_words[0].rearrange("p t r -> p (t r)").bitcast(I32))
-        plane_src = {"s1a": w1_scales[5:8, 0], "s3a": w3_scales[5:8, 0], "s2": w2_scales[:, 0], "s1b": w1_scales[0:5, 0], "s3b": w3_scales[0:5, 0]}
-        word_src = {"w1a": w1_words[6:7, 0], "w3a": w3_words[6:7, 0], "w2a": w2_words[5:8, 0], "w1b": w1_words[5:8:2, 0], "w3b": w3_words[5:8:2, 0],
-                    "w1c": w1_words[0:5, 0], "w3c": w3_words[0:5, 0], "w2c": w2_words[0:5, 0]}
+        plane_src = {"xs": x_scales, "s1": w1_scales[:, 0], "s3": w3_scales[:, 0], "s2": w2_scales[:, 0]}
+        word_src = {"w1": w1_words, "w3": w3_words, "w2": w2_words}
         W = {}
-        def load(name, e, tag=""):
-            if name == "xs":
-                for r in range(4):
-                    eng[e].dma_start(xs[:].bitcast(I32)[r:P:32, :], x_scales[0, r:16:4, :].bitcast(I32))
+
+        def load(item, tag=""):
+            name, lo, hi, step, e = item
+            if name == "xw":
+                eng[e].dma_start(xw[:], x_words[0].rearrange("p t r -> p (t r)").bitcast(I32))
             elif name in plane_src:
-                load_plane(eng[e], planes[name], plane_src[name])
+                load_plane([eng[c] for c in e], planes[name, lo], plane_src[name][lo:hi])
             elif name == "gates":
                 W[name] = keep.tile([P, 2, 2, T], F32, name="gates", tag=tag, align_bytes=64)
                 eng[e].dma_start(W[name][:].rearrange("p c h t -> p (c h) t"), gate.rearrange("c (h p) t -> p (c h) t", p=P))
             else:
-                W[name] = load_words(eng[e], name, word_src[name], tag)
-        for name, e in CFG["early"]:
-            load(name, e)
+                t = load_words(eng[e], "%s_%d" % (name, lo), word_src[name][lo:hi:step, 0], tag)
+                for k, x in enumerate(range(lo, hi, step)):
+                    W[name, x] = t[:, k, :]
+
+        for item in CFG["early"]:
+            load(item)
 
         def first_layer(e):
-            if e == 6:
-                return (W["w1a"][:, 0, :], s1a[:, 1, :]), (W["w3a"][:, 0, :], s3a[:, 1, :])
-            if e >= 5:
-                return (W["w1b"][:, (e - 5) // 2, :], s1a[:, e - 5, :]), (W["w3b"][:, (e - 5) // 2, :], s3a[:, e - 5, :])
-            return (W["w1c"][:, e, :], s1b[:, e, :]), (W["w3c"][:, e, :], s3b[:, e, :])
+            return (W["w1", e], plane_of["s1", e]), (W["w3", e], plane_of["s3", e])
 
         def second_layer(e, half):
-            words = W["w2a"][:, e - 5, :] if e >= 5 else W["w2c"][:, e, :]
-            return words[:, 2 * P * half : 2 * P * (half + 1)], s2[:, e, P * half : P * (half + 1)]
+            return W["w2", e][:, 2 * P * half : 2 * P * (half + 1)], plane_of["s2", e][:, P * half : P * (half + 1)]
 
         y = [keep.tile([P, S], F32, name="y%d" % half) for half in range(2)]
         tokens = {}
@@ -108,13 +101,15 @@ def tile_moe_rag_glu_relu_kernel(
         order = [s for group in GROUPS for s in group]
 
         def gather(g):
-            for piece in PIECES[g]:
+            for piece in PIECES:
+                if min(k for k in range(len(GROUPS)) if set(piece) & set(GROUPS[k])) != g:
+                    continue
                 n = P * len(piece)
                 cut = offs_t[:, 8 * piece[0] : 8 * piece[0] + n // 16]
                 words = ring.tile([P, n], U32, name="xg", bufs=CFG["xg"], align_bytes=64)
                 scales = ring.tile([P, n], U8, name="sg", bufs=CFG["sg"], align_bytes=64)
                 nc.vector.tensor_copy(words[:], xw[:].bitcast(U32).indirect(cut))
-                nc.vector.tensor_copy(scales[:], xs[:].indirect(cut))
+                nc.vector.tensor_copy(scales[:], xs[:, 0, :].indirect(cut))
                 for c, s in enumerate(piece):
                     tokens[s] = (words[:, P * c : P * (c + 1)], scales[:, P * c : P * (c + 1)])
 
@@ -132,13 +127,13 @@ def tile_moe_rag_glu_relu_kernel(
                 if place < len(CFG["late"]):
                     ra = keep.tile([P, H], F32, name="ra", tag="late%d" % place, align_bytes=64)
                 else:
-                    ra = ring.tile([P, H], F32, name="ra")
+                    ra = ring.tile([P, H], F32, name="ra", bufs=CFG["ra"])
                 nc.scalar.activation(
                     ra[:].rearrange("r (u p e) -> r u p e", u=2, e=2),
                     a[:].rearrange("r (p u e) -> r u p e", u=2, e=2),
                     RELU,
                 )
-                h = ring.tile([P, H], BF16, name="h", bufs=4)
+                h = ring.tile([P, H], BF16, name="h", bufs=12)
                 nc.vector.tensor_tensor(
                     h[:].rearrange("r (u p e) -> r u p e", u=2, e=2),
                     b[:].rearrange("r (p u e) -> r u p e", u=2, e=2),
@@ -149,28 +144,28 @@ def tile_moe_rag_glu_relu_kernel(
 
         def turn(g):
             m = len(GROUPS[g])
-            turned = psum.tile([P, m, 2, P], F32, name="turned", bufs=CFG["t"])
+            turned = psum.tile([P, m, 2, P], F32, name="turned", tag=CFG["tb"][g], bufs=CFG[CFG["tb"][g]])
             for c, s in enumerate(GROUPS[g]):
                 pairs = hidden[s][:].bitcast(F32)
                 for u in range(2):
                     nc.tensor.transpose(turned[:, c, u, :], pairs[:, P * u : P * (u + 1)], ident[:])
-            grouped = ring.tile([P, m * P * 4], BF16, name="grouped", align_bytes=64)
+            grouped = ring.tile([P, m * P * 4], BF16, name="grouped", bufs=4, align_bytes=64)
             (nc.vector.tensor_copy if CFG["tv"][g] else nc.scalar.copy)(
                 grouped[:].bitcast(F32).rearrange("p (c r u) -> p c r u", c=m, u=2),
                 turned[:].rearrange("p c u r -> p c r u"),
             )
-            codes = ring.tile([P, m * P], U32, name="codes", align_bytes=64)
-            scales = ring.tile([P, m * P], U8, name="scales", align_bytes=64)
+            codes = ring.tile([P, m * P], U32, name="codes", bufs=8, align_bytes=64)
+            scales = ring.tile([P, m * P], U8, name="scales", bufs=8, align_bytes=64)
             nc.vector.quantize_mx(out=codes[:].bitcast(FP8X4), scales=scales[:], in_=grouped[:])
             return codes, scales
 
         def project(g, codes, scales):
             group = GROUPS[g]
             m = len(group)
-            if CFG["yv"][g]:
+            if CFG["yv"][g] in (1, 2):
                 acc = [psum.tile([P, m * P], F32, name="acc", tag=CFG["ytag"][half], bufs=CFG[CFG["ytag"][half]])[:] for half in range(2)]
             else:
-                both = psum.tile([P, 2, m * P], F32, name="acc", tag="y", bufs=CFG["y"])
+                both = psum.tile([P, 2, m * P], F32, name="acc", tag=CFG["yb"][g], bufs=CFG[CFG["yb"][g]])
                 acc = [both[:, half, :] for half in range(2)]
             same = len(set(EXPERT_OF_TILE[s] for s in group)) == 1
             runs = [(group[0], 0, m * P)] if same else [(s, c * P, (c + 1) * P) for c, s in enumerate(group)]
@@ -187,14 +182,14 @@ def tile_moe_rag_glu_relu_kernel(
         G = len(GROUPS)
         made = {}
         done_late = 0
-        for step in range(-CFG["ga"], G + 2):
+        for step in range(-CFG["ga"], G + 8):
             for what in CFG["order"]:
                 if what == "g" and 0 <= step + CFG["ga"] < G:
                     gather(step + CFG["ga"])
-                if what == "l" and 0 <= step + 1 < G:
-                    gated(step + 1)
+                if what == "l" and 0 <= step + CFG["ll"] < G:
+                    gated(step + CFG["ll"])
                     while done_late < len(CFG["late"]) and order[done_late] in hidden:
-                        load(CFG["late"][done_late][0], CFG["late"][done_late][1], "late%d" % done_late)
+                        load(CFG["late"][done_late], "late%d" % done_late)
                         done_late += 1
                 if what == "t" and 0 <= step < G:
                     made[step] = turn(step)
@@ -218,6 +213,20 @@ def tile_moe_rag_glu_relu_kernel(
         def finish(i, terms):
             half, lo, hi = COMBINE[i]
             total = keep.tile([P, hi - lo], F32, name="total%d" % i)
+            if i < CFG["pe_add"]:
+                blocks = (hi - lo) // P
+                summed = psum.tile([P, blocks, P], F32, name="summed", tag="a", bufs=CFG["a"])
+                for c in range(blocks):
+                    for choice in range(2):
+                        nc.tensor.matmul(summed[:, c, :], terms[choice][:, P * c : P * (c + 1)], ident[:], start=choice == 0, stop=choice == 1, is_transpose=True)
+                across = ring.tile([P, blocks, P], F32, name="across")
+                nc.scalar.copy(across[:], summed[:])
+                back = psum.tile([P, blocks, P], F32, name="back", tag="b", bufs=CFG["b"])
+                for c in range(blocks):
+                    nc.tensor.transpose(back[:, c, :], across[:, c, :], ident[:])
+                nc.scalar.copy(total[:], back[:].rearrange("p c t -> p (c t)"))
+                nc.sync.dma_start(out[P * half : P * (half + 1), lo:hi], total[:])
+                return
             nc.vector.tensor_tensor(total[:], terms[0][:], terms[1][:], ADD)
             nc.sync.dma_start(out[P * half : P * (half + 1), lo:hi], total[:])
 

from contextlib import ExitStack

import concourse.mybir as mybir
from concourse.masks import make_identity

K, T, E, H, N = 512, 768, 8, 512, 256
COUNTS = (128, 128, 128, 128, 128, 256, 512, 128)
S = sum(COUNTS)
FLOPS = 2 * S * (2 * K * H + H * N)

F32 = mybir.dt.float32
BF16 = mybir.dt.bfloat16
I32 = mybir.dt.int32
U32 = mybir.dt.uint32
U16 = mybir.dt.uint16
U8 = mybir.dt.uint8
FP8X4 = mybir.dt.float8_e4m3fn_x4
FP4X4 = mybir.dt.float4_e2m1fn_x4
MULT = mybir.AluOpType.mult
ADD = mybir.AluOpType.add
RELU = mybir.ActivationFunctionType.Relu

P = 128
EXPERT_OF_TILE = [e for e in range(E) for c in range(COUNTS[e] // P)]
CFG = {"combine":[[0,0,768],[1,0,384],[1,384,768]],"tail":[[0,0],[1,0],[0,1],[2,0],[1,1],[0,2],[1,2],[2,1],[2,2]],"xg":4,"sg":5,"a":2,"b":3,"t":1,"y":2,"ytag":["a","b"],"ga":4,"pl":6,"ll":2,"order":["t","g","l","p"],"pe_add":0,"groups":[[9,10],[7,8],[5,6],[11],[3,4],[1,2],[0]],"pieces":[[9],[10,11],[7,8],[5,6],[3,4],[1,2],[0]],"tv":[0,0,0,0,0,0,0],"yv":[0,3,0,0,3,3,0],"zero":[["s1",5,8,"v"],["xs",0,1,"v"],["s3",5,8,"v"],["s2",0,8,"v"],["s1",0,5,"g"],["s3",0,5,"v"]],"early":[["xw",0,0,1,"s"],["xs",0,1,1,"ssss"],["w1",6,7,1,"s"],["s3",5,8,1,"aaaa"],["w3",6,7,1,"s"],["s1",5,8,1,"aaaa"],["w2",5,8,1,"s"],["s2",0,8,1,"ssss"],["w3",5,8,2,"s"],["w1",5,8,2,"s"],["s1",0,5,1,"aaaa"],["s3",0,5,1,"aaaa"],["w1",0,5,1,"s"]],"late":[["w3",0,5,1,"s"],["w2",0,5,1,"s"],["gates",0,0,1,"s"]],"kind":"K","ra":6,"yb":["y","y","y","t","b","a","y"],"tb":["t","t","t","t","t","a","a"]}
GROUPS = CFG["groups"]
PIECES = CFG["pieces"]
COMBINE = CFG["combine"]


def tile_moe_rag_glu_relu_kernel(
    tc, x_words, x_scales, w1_words, w1_scales, w3_words, w3_scales, w2_words, w2_scales, gate, offs, pos1, pos2, out
):
    nc = tc.nc
    with ExitStack() as ctx:
        keep = ctx.enter_context(tc.tile_pool(name="keep", bufs=1))
        ring = ctx.enter_context(tc.tile_pool(name="ring", bufs=3))
        psum = ctx.enter_context(tc.psum_pool(name="psum", bufs=1))

        def load_plane(queue, plane, scales):
            for r in range(4):
                queue[r].dma_start(
                    plane[:].bitcast(I32)[r:P:32, :, :],
                    scales[:, r:16:4, :].rearrange("e q c -> q e c").bitcast(I32),
                )

        def load_words(queue, name, words, tag=""):
            tile = keep.tile([P, words.shape[0], words.shape[2]], U8, name=name, tag=tag, align_bytes=64)
            queue.dma_start(tile[:].bitcast(I32), words.rearrange("e p c -> p e c").bitcast(I32))
            return tile

        warm = keep.tile([P, 2], F32, name="warm")
        nc.vector.memset(warm[:, 0:1], 0.0)
        nc.scalar.activation(warm[:, 1:2], warm[:, 0:1], RELU)
        eng = {"v": nc.vector, "g": nc.gpsimd, "s": nc.sync, "a": nc.scalar}
        planes = {}
        plane_of = {}
        for name, lo, hi, e in CFG["zero"]:
            t = keep.tile([P, hi - lo, {"xs": T, "s1": H, "s3": H, "s2": N}[name]], U8, name="%s_%d" % (name, lo), align_bytes=64)
            eng[e].memset(t[:].bitcast(I32), 0)
            planes[name, lo] = t
            for x in range(lo, hi):
                plane_of[name, x] = t[:, x - lo, :]
        xs = planes["xs", 0]
        ident = keep.tile([P, P], F32, name="ident")
        make_identity(nc, ident[:])

        offs_t = keep.tile([P, S // 16], U16, name="offs_t")
        nc.sync.dma_start(offs_t[:], offs)
        xw = keep.tile([P, T], I32, name="xw", align_bytes=64)
        plane_src = {"xs": x_scales, "s1": w1_scales[:, 0], "s3": w3_scales[:, 0], "s2": w2_scales[:, 0]}
        word_src = {"w1": w1_words, "w3": w3_words, "w2": w2_words}
        W = {}

        def load(item, tag=""):
            name, lo, hi, step, e = item
            if name == "xw":
                eng[e].dma_start(xw[:], x_words[0].rearrange("p t r -> p (t r)").bitcast(I32))
            elif name in plane_src:
                load_plane([eng[c] for c in e], planes[name, lo], plane_src[name][lo:hi])
            elif name == "gates":
                W[name] = keep.tile([P, 2, 2, T], F32, name="gates", tag=tag, align_bytes=64)
                eng[e].dma_start(W[name][:].rearrange("p c h t -> p (c h) t"), gate.rearrange("c (h p) t -> p (c h) t", p=P))
            else:
                t = load_words(eng[e], "%s_%d" % (name, lo), word_src[name][lo:hi:step, 0], tag)
                for k, x in enumerate(range(lo, hi, step)):
                    W[name, x] = t[:, k, :]

        for item in CFG["early"]:
            load(item)

        def first_layer(e):
            return (W["w1", e], plane_of["s1", e]), (W["w3", e], plane_of["s3", e])

        def second_layer(e, half):
            return W["w2", e][:, 2 * P * half : 2 * P * (half + 1)], plane_of["s2", e][:, P * half : P * (half + 1)]

        y = [keep.tile([P, S], F32, name="y%d" % half) for half in range(2)]
        tokens = {}
        hidden = {}
        order = [s for group in GROUPS for s in group]

        def gather(g):
            for piece in PIECES:
                if min(k for k in range(len(GROUPS)) if set(piece) & set(GROUPS[k])) != g:
                    continue
                n = P * len(piece)
                cut = offs_t[:, 8 * piece[0] : 8 * piece[0] + n // 16]
                words = ring.tile([P, n], U32, name="xg", bufs=CFG["xg"], align_bytes=64)
                scales = ring.tile([P, n], U8, name="sg", bufs=CFG["sg"], align_bytes=64)
                nc.vector.tensor_copy(words[:], xw[:].bitcast(U32).indirect(cut))
                nc.vector.tensor_copy(scales[:], xs[:, 0, :].indirect(cut))
                for c, s in enumerate(piece):
                    tokens[s] = (words[:, P * c : P * (c + 1)], scales[:, P * c : P * (c + 1)])

        def gated(g):
            for s in GROUPS[g]:
                words, scales = tokens[s]
                a = psum.tile([P, H], F32, name="a", bufs=CFG["a"])
                b = psum.tile([P, H], F32, name="b", bufs=CFG["b"])
                for acc, (w, ws) in zip((a, b), first_layer(EXPERT_OF_TILE[s])):
                    nc.tensor.matmul_mx(
                        out=acc[:], lhsT=words.bitcast(FP8X4), lhsT_scale=scales,
                        rhs=w.bitcast(FP4X4), rhs_scale=ws, start=True, stop=True,
                    )
                place = order.index(s)
                if place < len(CFG["late"]):
                    ra = keep.tile([P, H], F32, name="ra", tag="late%d" % place, align_bytes=64)
                else:
                    ra = ring.tile([P, H], F32, name="ra", bufs=CFG["ra"])
                nc.scalar.activation(
                    ra[:].rearrange("r (u p e) -> r u p e", u=2, e=2),
                    a[:].rearrange("r (p u e) -> r u p e", u=2, e=2),
                    RELU,
                )
                h = ring.tile([P, H], BF16, name="h", bufs=12)
                nc.vector.tensor_tensor(
                    h[:].rearrange("r (u p e) -> r u p e", u=2, e=2),
                    b[:].rearrange("r (p u e) -> r u p e", u=2, e=2),
                    ra[:].rearrange("r (u p e) -> r u p e", u=2, e=2),
                    MULT,
                )
                hidden[s] = h

        def turn(g):
            m = len(GROUPS[g])
            turned = psum.tile([P, m, 2, P], F32, name="turned", tag=CFG["tb"][g], bufs=CFG[CFG["tb"][g]])
            for c, s in enumerate(GROUPS[g]):
                pairs = hidden[s][:].bitcast(F32)
                for u in range(2):
                    nc.tensor.transpose(turned[:, c, u, :], pairs[:, P * u : P * (u + 1)], ident[:])
            grouped = ring.tile([P, m * P * 4], BF16, name="grouped", bufs=4, align_bytes=64)
            (nc.vector.tensor_copy if CFG["tv"][g] else nc.scalar.copy)(
                grouped[:].bitcast(F32).rearrange("p (c r u) -> p c r u", c=m, u=2),
                turned[:].rearrange("p c u r -> p c r u"),
            )
            codes = ring.tile([P, m * P], U32, name="codes", bufs=8, align_bytes=64)
            scales = ring.tile([P, m * P], U8, name="scales", bufs=8, align_bytes=64)
            nc.vector.quantize_mx(out=codes[:].bitcast(FP8X4), scales=scales[:], in_=grouped[:])
            return codes, scales

        def project(g, codes, scales):
            group = GROUPS[g]
            m = len(group)
            if CFG["yv"][g] in (1, 2):
                acc = [psum.tile([P, m * P], F32, name="acc", tag=CFG["ytag"][half], bufs=CFG[CFG["ytag"][half]])[:] for half in range(2)]
            else:
                both = psum.tile([P, 2, m * P], F32, name="acc", tag=CFG["yb"][g], bufs=CFG[CFG["yb"][g]])
                acc = [both[:, half, :] for half in range(2)]
            same = len(set(EXPERT_OF_TILE[s] for s in group)) == 1
            runs = [(group[0], 0, m * P)] if same else [(s, c * P, (c + 1) * P) for c, s in enumerate(group)]
            for half in range(2):
                for s, lo, hi in runs:
                    w, ws = second_layer(EXPERT_OF_TILE[s], half)
                    nc.tensor.matmul_mx(
                        out=acc[half][:, lo:hi], lhsT=w.bitcast(FP4X4), lhsT_scale=ws,
                        rhs=codes[:, lo:hi].bitcast(FP8X4), rhs_scale=scales[:, lo:hi], start=True, stop=True,
                    )
            for half in range(2):
                (nc.vector.tensor_copy if CFG["yv"][g] in (half + 1, 3) else nc.scalar.copy)(y[half][:, P * group[0] : P * (group[0] + m)], acc[half])

        G = len(GROUPS)
        made = {}
        done_late = 0
        for step in range(-CFG["ga"], G + 8):
            for what in CFG["order"]:
                if what == "g" and 0 <= step + CFG["ga"] < G:
                    gather(step + CFG["ga"])
                if what == "l" and 0 <= step + CFG["ll"] < G:
                    gated(step + CFG["ll"])
                    while done_late < len(CFG["late"]) and order[done_late] in hidden:
                        load(CFG["late"][done_late], "late%d" % done_late)
                        done_late += 1
                if what == "t" and 0 <= step < G:
                    made[step] = turn(step)
                if what == "p" and 0 <= step - CFG["pl"] < G:
                    project(step - CFG["pl"], *made[step - CFG["pl"]])

        pos_t = []
        for name, pos in (("pos1_t", pos1), ("pos2_t", pos2)):
            t = keep.tile([P, T // 16], U16, name=name)
            nc.sync.dma_start(t[:], pos)
            pos_t.append(t)

        def weighted(i, choice):
            half, lo, hi = COMBINE[i]
            t = keep.tile([P, hi - lo], F32, name="term%d_%d" % (i, choice))
            nc.vector.tensor_tensor(
                t[:], y[half][:].indirect(pos_t[choice][:, lo // 16 : hi // 16]), W["gates"][:, choice, half, lo:hi], MULT
            )
            return t

        def finish(i, terms):
            half, lo, hi = COMBINE[i]
            total = keep.tile([P, hi - lo], F32, name="total%d" % i)
            if i < CFG["pe_add"]:
                blocks = (hi - lo) // P
                summed = psum.tile([P, blocks, P], F32, name="summed", tag="a", bufs=CFG["a"])
                for c in range(blocks):
                    for choice in range(2):
                        nc.tensor.matmul(summed[:, c, :], terms[choice][:, P * c : P * (c + 1)], ident[:], start=choice == 0, stop=choice == 1, is_transpose=True)
                across = ring.tile([P, blocks, P], F32, name="across")
                nc.scalar.copy(across[:], summed[:])
                back = psum.tile([P, blocks, P], F32, name="back", tag="b", bufs=CFG["b"])
                for c in range(blocks):
                    nc.tensor.transpose(back[:, c, :], across[:, c, :], ident[:])
                nc.scalar.copy(total[:], back[:].rearrange("p c t -> p (c t)"))
                nc.sync.dma_start(out[P * half : P * (half + 1), lo:hi], total[:])
                return
            nc.vector.tensor_tensor(total[:], terms[0][:], terms[1][:], ADD)
            nc.sync.dma_start(out[P * half : P * (half + 1), lo:hi], total[:])

        terms = {}
        for kind, i in CFG["tail"]:
            if kind == 2:
                finish(i, (terms[i, 0], terms[i, 1]))
            else:
                terms[i, kind] = weighted(i, kind)
